import numpy as np, ml_dtypes
CORES = [44,45,46,47,172,173,174,175,300,301,302,303,428,429,430,431]
N = 16
TK = 32
def setup_inputs(rng):
    return {"x": rng.standard_normal((N, 128, N * TK), dtype=np.float32).astype(ml_dtypes.bfloat16), "t": rng.standard_normal((N, 128, N * TK), dtype=np.float32).astype(ml_dtypes.bfloat16), "f1": (rng.standard_normal((N, 128, 128), dtype=np.float32) / 11).astype(ml_dtypes.bfloat16), "f2": (rng.standard_normal((N, 128, 128), dtype=np.float32) / 11).astype(ml_dtypes.bfloat16)}
def setup_inputs_big(rng):
    d = setup_inputs(rng)
    for k in ("x", "t", "f1", "f2"): d[k] = (d[k].astype(np.float32) * 1024.0).astype(d[k].dtype)
    return d
def setup_inputs_small(rng):
    d = setup_inputs(rng)
    for k in ("x", "t", "f1", "f2"): d[k] = (d[k].astype(np.float32) * (1 / 1024.0)).astype(d[k].dtype)
    return d
def reference(x, t, f1, f2):
    X, T, F1, F2 = x.astype(np.float64), t.astype(np.float64), f1.astype(np.float64), f2.astype(np.float64)
    y = np.zeros((N, 128, N * TK))
    for j in range(N):
        u = (F1[j].T @ X[j]) * T[j]
        for r in range(N):
            y[r][:, TK * j:TK * j + TK] = F2[r].T @ u[:, TK * r:TK * r + TK]
    return {"y": y.astype(ml_dtypes.bfloat16)}

@@ -1,0 +1,164 @@
+from concourse.bass import DstId, RemoteDMATransfer
+from concourse.mybir import AluOpType
+
+TK = 32
+NB = 16
+HALF = NB // 2 * TK
+
+SCRATCH = {
+    "f1s": ("sbuf", [128, 128], "bfloat16"),
+    "f2s": ("sbuf", [128, 128], "bfloat16"),
+    "xs": ("sbuf", [128, NB * TK], "bfloat16"),
+    "ts": ("sbuf", [128, NB * TK], "bfloat16"),
+    "u": ("sbuf", [128, NB * TK], "bfloat16"),
+    "tr": ("sbuf", [128, HALF], "bfloat16"),
+    "land": ("sbuf", [128, NB * TK], "bfloat16"),
+    "yb": ("sbuf", [128, NB * TK], "bfloat16"),
+    "p1f": ("psum", [128, 512], "float32"),
+    "p1n": ("psum", [128, 512], "float32"),
+    "p2n": ("psum", [128, 512], "float32"),
+    "p2f": ("psum", [128, 512], "float32"),
+}
+SEMAPHORES = ["l_f1", "l_f2", "l_xf", "l_tf", "l_xn", "l_tn", "m1f", "m1n", "uf", "un", "own", "trk", "arr1", "arr2",
+              "cp", "m2n", "m2f", "yn", "yf", "stn", "stf", "sent"]
+
+
+def _bits(mask):
+    return [e for e in range(mask.bit_length()) if (mask >> e) & 1]
+
+
+def _mask(engines):
+    m = 0
+    for e in engines:
+        m |= 1 << e
+    return m
+
+
+def _place(c, cores, topo):
+    by_host = {}
+    for d in cores:
+        by_host.setdefault(topo.host(d), []).append(d)
+    here = by_host[topo.host(c)]
+    p = {"k": here.index(c), "local": [d for d in here if d != c]}
+    for h, members in by_host.items():
+        if h == topo.host(c):
+            continue
+        if not topo.may_write(c, members[0]):
+            p["diag"] = members
+        elif topo.same_plane(c, members[0]):
+            p["plane"] = members
+        else:
+            p["cable"] = members
+    near = sorted(cores.index(d) for d in here + p["plane"])
+    far = sorted(cores.index(d) for d in p["cable"] + p["diag"])
+    assert near == list(range(near[0], near[0] + len(near))) and far == list(range(far[0], far[0] + len(far)))
+    p["near0"], p["far0"] = near[0] * TK, far[0] * TK
+    return p
+
+
+def _plan(c, cores, topo):
+    p = _place(c, cores, topo)
+    me = cores.index(c)
+    peer = p["cable"][p["k"]]
+    off = _bits(topo.mask(c, peer))
+    on = [e for e in _bits(topo.mask(c, p["local"][0])) if e not in off]
+    trunk = [(peer, "u", p["far0"], "tr", 0, HALF, off, "trk")]
+
+    def spread(src, col_of, dst_col, sem):
+        out = []
+        n_off = len(off) // len(p["plane"])
+        for i, d in enumerate(p["plane"]):
+            out.append((d, src, col_of(d), "land", dst_col, TK, off[i * n_off:(i + 1) * n_off], sem))
+        n_on = 1
+        while n_on * 2 * len(p["local"]) <= len(on):
+            n_on *= 2
+        for i, d in enumerate(p["local"]):
+            out.append((d, src, col_of(d), "land", dst_col, TK, on[i * n_on:(i + 1) * n_on], sem))
+        return out
+
+    near = spread("u", lambda d: cores.index(d) * TK, me * TK, "arr1")
+    scatter = spread("tr", lambda d: cores.index(d) * TK - p["near0"], cores.index(peer) * TK, "arr2")
+    return [trunk, near, scatter]
+
+
+def rank_program(g, core, T, topo):
+    if T.rank_of(core) is None:
+        return
+    cores = list(T.cores)
+    S = T.sem
+    pe, ve = g.tensor, g.vector
+    p = _place(core, cores, topo)
+    me = cores.index(core)
+    peer = p["cable"][p["k"]]
+    far = slice(p["far0"], p["far0"] + HALF)
+    near = slice(p["near0"], p["near0"] + HALF)
+    calls = _plan(core, cores, topo)
+    expect = {"trk": 0, "arr1": 0, "arr2": 0}
+    for d in cores:
+        if d != core:
+            for call in _plan(d, cores, topo):
+                for w in call:
+                    if w[0] == core:
+                        expect[w[7]] += len(w[6])
+
+    def issue(call):
+        trs = []
+        for (d, sb, sc, db, dc, n, engines, sem) in call:
+            rid, pid = topo.addr(d, core)
+            trs.append(RemoteDMATransfer(dst_ids=[DstId(rid=rid, pnc=pid)], dma_engine_mask=_mask(engines),
+                                         remote_sem=S[sem], src=T[sb][:, sc:sc + n], dst=T[db][:, dc:dc + n]))
+        g.remote_dma_fused(trs, local_sem=S.sent)
+        return sum(len(w[6]) for w in call)
+
+    g.sync.dma_start(T.f1s[:], T.f1[:]).then_inc(S.l_f1, 16)
+    g.scalar.dma_start(T.xs[:, far], T.x[:, far]).then_inc(S.l_xf, 16)
+    g.sync.dma_start(T.ts[:, far], T.t[:, far]).then_inc(S.l_tf, 16)
+    g.scalar.dma_start(T.xs[:, near], T.x[:, near]).then_inc(S.l_xn, 16)
+    g.sync.dma_start(T.ts[:, near], T.t[:, near]).then_inc(S.l_tn, 16)
+    g.scalar.dma_start(T.f2s[:], T.f2[:]).then_inc(S.l_f2, 16)
+
+    pe.wait_ge(S.l_f1, 16)
+    pe.wait_ge(S.l_xf, 16)
+    pe.matmul(T.p1f[:, 0:HALF], T.f1s[:], T.xs[:, far], start=True, stop=True).then_inc(S.m1f, 1)
+    pe.wait_ge(S.l_xn, 16)
+    pe.matmul(T.p1n[:, 0:HALF], T.f1s[:], T.xs[:, near], start=True, stop=True).then_inc(S.m1n, 1)
+    ve.wait_ge(S.m1f, 1)
+    ve.wait_ge(S.l_tf, 16)
+    ve.tensor_tensor(T.u[:, far], T.p1f[:, 0:HALF], T.ts[:, far], AluOpType.mult).then_inc(S.uf, 1)
+    ve.wait_ge(S.m1n, 1)
+    ve.wait_ge(S.l_tn, 16)
+    ve.tensor_tensor(T.u[:, near], T.p1n[:, 0:HALF], T.ts[:, near], AluOpType.mult).then_inc(S.un, 1)
+    o = me * TK
+    ve.tensor_tensor(T.land[:, o:o + TK], T.p1n[:, o - p["near0"]:o - p["near0"] + TK], T.ts[:, o:o + TK],
+                     AluOpType.mult).then_inc(S.own, 1)
+
+    sent = 0
+    g.wait_ge(S.uf, 1)
+    sent += issue(calls[0])
+    g.wait_ge(S.un, 1)
+    sent += issue(calls[1])
+    g.wait_ge(S.trk, expect["trk"])
+    sent += issue(calls[2])
+
+    q = cores.index(peer) * TK
+    ve.wait_ge(S.trk, expect["trk"])
+    ve.tensor_copy(T.land[:, q:q + TK], T.tr[:, o - p["near0"]:o - p["near0"] + TK]).then_inc(S.cp, 1)
+
+    pe.wait_ge(S.l_f2, 16)
+    pe.wait_ge(S.own, 1)
+    pe.wait_ge(S.arr1, expect["arr1"])
+    pe.matmul(T.p2n[:, 0:HALF], T.f2s[:], T.land[:, near], start=True, stop=True).then_inc(S.m2n, 1)
+    pe.wait_ge(S.cp, 1)
+    pe.wait_ge(S.arr2, expect["arr2"])
+    pe.matmul(T.p2f[:, 0:HALF], T.f2s[:], T.land[:, far], start=True, stop=True).then_inc(S.m2f, 1)
+    ve.wait_ge(S.m2n, 1)
+    ve.tensor_copy(T.yb[:, near], T.p2n[:, 0:HALF]).then_inc(S.yn, 1)
+    ve.wait_ge(S.m2f, 1)
+    ve.tensor_copy(T.yb[:, far], T.p2f[:, 0:HALF]).then_inc(S.yf, 1)
+    g.sync.wait_ge(S.yn, 1)
+    g.sync.dma_start(T.y[:, near], T.yb[:, near]).then_inc(S.stn, 16)
+    g.scalar.wait_ge(S.yf, 1)
+    g.scalar.dma_start(T.y[:, far], T.yb[:, far]).then_inc(S.stf, 16)
+    g.sync.wait_ge(S.stn, 16)
+    g.scalar.wait_ge(S.stf, 16)
+    g.wait_ge(S.sent, sent)

@@ -4,6 +4,7 @@ from concourse.mybir import AluOpType
 TK = 32
 NB = 16
 HALF = NB // 2 * TK
+QUART = NB // 4 * TK
 
 SCRATCH = {
     "f1s": ("sbuf", [128, 128], "bfloat16"),
@@ -11,16 +12,18 @@ SCRATCH = {
     "xs": ("sbuf", [128, NB * TK], "bfloat16"),
     "ts": ("sbuf", [128, NB * TK], "bfloat16"),
     "u": ("sbuf", [128, NB * TK], "bfloat16"),
-    "tr": ("sbuf", [128, HALF], "bfloat16"),
+    "tr": ("sbuf", [128, QUART], "bfloat16"),
     "land": ("sbuf", [128, NB * TK], "bfloat16"),
     "yb": ("sbuf", [128, NB * TK], "bfloat16"),
-    "p1f": ("psum", [128, 512], "float32"),
+    "p1d": ("psum", [128, 512], "float32"),
+    "p1c": ("psum", [128, 512], "float32"),
     "p1n": ("psum", [128, 512], "float32"),
+    "p2d": ("psum", [128, 512], "float32"),
+    "p2c": ("psum", [128, 512], "float32"),
     "p2n": ("psum", [128, 512], "float32"),
-    "p2f": ("psum", [128, 512], "float32"),
 }
-SEMAPHORES = ["l_f1", "l_f2", "l_xf", "l_tf", "l_xn", "l_tn", "m1f", "m1n", "uf", "un", "own", "trk", "arr1", "arr2",
-              "cp", "m2n", "m2f", "yn", "yf", "stn", "stf", "sent"]
+SEMAPHORES = ["l_f1", "l_f2", "l_xd", "l_td", "l_xc", "l_tc", "l_xn", "l_tn", "m1d", "m1c", "m1n", "ud", "uc", "un", "own",
+              "trk", "arrc", "arrn", "arrd", "m2d", "m2c", "m2n", "yd", "yc", "yn", "std", "stc", "stn", "sent"]
 
 
 def _bits(mask):
@@ -49,36 +52,37 @@ def _place(c, cores, topo):
             p["plane"] = members
         else:
             p["cable"] = members
-    near = sorted(cores.index(d) for d in here + p["plane"])
-    far = sorted(cores.index(d) for d in p["cable"] + p["diag"])
-    assert near == list(range(near[0], near[0] + len(near))) and far == list(range(far[0], far[0] + len(far)))
-    p["near0"], p["far0"] = near[0] * TK, far[0] * TK
+
+    def first_col(members):
+        r = sorted(cores.index(d) for d in members)
+        assert r == list(range(r[0], r[0] + len(r)))
+        return r[0] * TK
+
+    p["near0"], p["dg0"], p["cb0"], p["pl0"] = (first_col(here + p["plane"]), first_col(p["diag"]), first_col(p["cable"]),
+                                                first_col(p["plane"]))
+    first, second = ("plane", "cable") if p["k"] % 2 == 0 else ("cable", "plane")
+    p["relay"], p["beyond"], p["beyond0"] = p[first][p["k"]], p[second], first_col(p[second])
     return p
 
 
 def _plan(c, cores, topo):
     p = _place(c, cores, topo)
     me = cores.index(c)
-    peer = p["cable"][p["k"]]
-    off = _bits(topo.mask(c, peer))
+    off = _bits(topo.mask(c, p["relay"]))
     on = [e for e in _bits(topo.mask(c, p["local"][0])) if e not in off]
-    trunk = [(peer, "u", p["far0"], "tr", 0, HALF, off, "trk")]
 
-    def spread(src, col_of, dst_col, sem):
-        out = []
-        n_off = len(off) // len(p["plane"])
-        for i, d in enumerate(p["plane"]):
-            out.append((d, src, col_of(d), "land", dst_col, TK, off[i * n_off:(i + 1) * n_off], sem))
-        n_on = 1
-        while n_on * 2 * len(p["local"]) <= len(on):
-            n_on *= 2
-        for i, d in enumerate(p["local"]):
-            out.append((d, src, col_of(d), "land", dst_col, TK, on[i * n_on:(i + 1) * n_on], sem))
-        return out
+    def spread(dsts, engines, src, col0, dst_col, sem):
+        n = 1
+        while n * 2 * len(dsts) <= len(engines):
+            n *= 2
+        return [(d, src, cores.index(d) * TK - col0, "land", dst_col, TK, engines[i * n:(i + 1) * n], sem)
+                for i, d in enumerate(dsts)]
 
-    near = spread("u", lambda d: cores.index(d) * TK, me * TK, "arr1")
-    scatter = spread("tr", lambda d: cores.index(d) * TK - p["near0"], cores.index(peer) * TK, "arr2")
-    return [trunk, near, scatter]
+    trunk = [(p["relay"], "u", p["dg0"], "tr", 0, QUART, off, "trk")]
+    cable = spread(p["cable"], off, "u", 0, me * TK, "arrc")
+    near = spread(p["plane"], off, "u", 0, me * TK, "arrn") + spread(p["local"], on, "u", 0, me * TK, "arrn")
+    scatter = spread(p["beyond"], off, "tr", p["beyond0"], cores.index(p["relay"]) * TK, "arrd")
+    return [trunk, cable, near, scatter]
 
 
 def rank_program(g, core, T, topo):
@@ -89,11 +93,11 @@ def rank_program(g, core, T, topo):
     pe, ve = g.tensor, g.vector
     p = _place(core, cores, topo)
     me = cores.index(core)
-    peer = p["cable"][p["k"]]
-    far = slice(p["far0"], p["far0"] + HALF)
+    dg = slice(p["dg0"], p["dg0"] + QUART)
+    cb = slice(p["cb0"], p["cb0"] + QUART)
     near = slice(p["near0"], p["near0"] + HALF)
     calls = _plan(core, cores, topo)
-    expect = {"trk": 0, "arr1": 0, "arr2": 0}
+    expect = {"trk": 0, "arrc": 0, "arrn": 0, "arrd": 0}
     for d in cores:
         if d != core:
             for call in _plan(d, cores, topo):
@@ -111,20 +115,27 @@ def rank_program(g, core, T, topo):
         return sum(len(w[6]) for w in call)
 
     g.sync.dma_start(T.f1s[:], T.f1[:]).then_inc(S.l_f1, 16)
-    g.scalar.dma_start(T.xs[:, far], T.x[:, far]).then_inc(S.l_xf, 16)
-    g.sync.dma_start(T.ts[:, far], T.t[:, far]).then_inc(S.l_tf, 16)
+    g.scalar.dma_start(T.xs[:, dg], T.x[:, dg]).then_inc(S.l_xd, 16)
+    g.sync.dma_start(T.ts[:, dg], T.t[:, dg]).then_inc(S.l_td, 16)
+    g.scalar.dma_start(T.xs[:, cb], T.x[:, cb]).then_inc(S.l_xc, 16)
+    g.sync.dma_start(T.ts[:, cb], T.t[:, cb]).then_inc(S.l_tc, 16)
     g.scalar.dma_start(T.xs[:, near], T.x[:, near]).then_inc(S.l_xn, 16)
     g.sync.dma_start(T.ts[:, near], T.t[:, near]).then_inc(S.l_tn, 16)
     g.scalar.dma_start(T.f2s[:], T.f2[:]).then_inc(S.l_f2, 16)
 
     pe.wait_ge(S.l_f1, 16)
-    pe.wait_ge(S.l_xf, 16)
-    pe.matmul(T.p1f[:, 0:HALF], T.f1s[:], T.xs[:, far], start=True, stop=True).then_inc(S.m1f, 1)
+    pe.wait_ge(S.l_xd, 16)
+    pe.matmul(T.p1d[:, 0:QUART], T.f1s[:], T.xs[:, dg], start=True, stop=True).then_inc(S.m1d, 1)
+    pe.wait_ge(S.l_xc, 16)
+    pe.matmul(T.p1c[:, 0:QUART], T.f1s[:], T.xs[:, cb], start=True, stop=True).then_inc(S.m1c, 1)
     pe.wait_ge(S.l_xn, 16)
     pe.matmul(T.p1n[:, 0:HALF], T.f1s[:], T.xs[:, near], start=True, stop=True).then_inc(S.m1n, 1)
-    ve.wait_ge(S.m1f, 1)
-    ve.wait_ge(S.l_tf, 16)
-    ve.tensor_tensor(T.u[:, far], T.p1f[:, 0:HALF], T.ts[:, far], AluOpType.mult).then_inc(S.uf, 1)
+    ve.wait_ge(S.m1d, 1)
+    ve.wait_ge(S.l_td, 16)
+    ve.tensor_tensor(T.u[:, dg], T.p1d[:, 0:QUART], T.ts[:, dg], AluOpType.mult).then_inc(S.ud, 1)
+    ve.wait_ge(S.m1c, 1)
+    ve.wait_ge(S.l_tc, 16)
+    ve.tensor_tensor(T.u[:, cb], T.p1c[:, 0:QUART], T.ts[:, cb], AluOpType.mult).then_inc(S.uc, 1)
     ve.wait_ge(S.m1n, 1)
     ve.wait_ge(S.l_tn, 16)
     ve.tensor_tensor(T.u[:, near], T.p1n[:, 0:HALF], T.ts[:, near], AluOpType.mult).then_inc(S.un, 1)
@@ -133,32 +144,36 @@ def rank_program(g, core, T, topo):
                      AluOpType.mult).then_inc(S.own, 1)
 
     sent = 0
-    g.wait_ge(S.uf, 1)
+    g.wait_ge(S.ud, 1)
     sent += issue(calls[0])
-    g.wait_ge(S.un, 1)
+    g.wait_ge(S.uc, 1)
     sent += issue(calls[1])
-    g.wait_ge(S.trk, expect["trk"])
+    g.wait_ge(S.un, 1)
     sent += issue(calls[2])
-
-    q = cores.index(peer) * TK
-    ve.wait_ge(S.trk, expect["trk"])
-    ve.tensor_copy(T.land[:, q:q + TK], T.tr[:, o - p["near0"]:o - p["near0"] + TK]).then_inc(S.cp, 1)
+    g.wait_ge(S.trk, expect["trk"])
+    sent += issue(calls[3])
 
     pe.wait_ge(S.l_f2, 16)
+    pe.wait_ge(S.arrc, expect["arrc"])
+    pe.matmul(T.p2c[:, 0:QUART], T.f2s[:], T.land[:, cb], start=True, stop=True).then_inc(S.m2c, 1)
     pe.wait_ge(S.own, 1)
-    pe.wait_ge(S.arr1, expect["arr1"])
+    pe.wait_ge(S.arrn, expect["arrn"])
     pe.matmul(T.p2n[:, 0:HALF], T.f2s[:], T.land[:, near], start=True, stop=True).then_inc(S.m2n, 1)
-    pe.wait_ge(S.cp, 1)
-    pe.wait_ge(S.arr2, expect["arr2"])
-    pe.matmul(T.p2f[:, 0:HALF], T.f2s[:], T.land[:, far], start=True, stop=True).then_inc(S.m2f, 1)
+    pe.wait_ge(S.arrd, expect["arrd"])
+    pe.matmul(T.p2d[:, 0:QUART], T.f2s[:], T.land[:, dg], start=True, stop=True).then_inc(S.m2d, 1)
+    ve.wait_ge(S.m2c, 1)
+    ve.tensor_copy(T.yb[:, cb], T.p2c[:, 0:QUART]).then_inc(S.yc, 1)
     ve.wait_ge(S.m2n, 1)
     ve.tensor_copy(T.yb[:, near], T.p2n[:, 0:HALF]).then_inc(S.yn, 1)
-    ve.wait_ge(S.m2f, 1)
-    ve.tensor_copy(T.yb[:, far], T.p2f[:, 0:HALF]).then_inc(S.yf, 1)
-    g.sync.wait_ge(S.yn, 1)
-    g.sync.dma_start(T.y[:, near], T.yb[:, near]).then_inc(S.stn, 16)
-    g.scalar.wait_ge(S.yf, 1)
-    g.scalar.dma_start(T.y[:, far], T.yb[:, far]).then_inc(S.stf, 16)
-    g.sync.wait_ge(S.stn, 16)
-    g.scalar.wait_ge(S.stf, 16)
+    ve.wait_ge(S.m2d, 1)
+    ve.tensor_copy(T.yb[:, dg], T.p2d[:, 0:QUART]).then_inc(S.yd, 1)
+    g.sync.wait_ge(S.yc, 1)
+    g.sync.dma_start(T.y[:, cb], T.yb[:, cb]).then_inc(S.stc, 16)
+    g.scalar.wait_ge(S.yn, 1)
+    g.scalar.dma_start(T.y[:, near], T.yb[:, near]).then_inc(S.stn, 16)
+    g.sync.wait_ge(S.yd, 1)
+    g.sync.dma_start(T.y[:, dg], T.yb[:, dg]).then_inc(S.std, 16)
+    g.scalar.wait_ge(S.stn, 16)
+    g.sync.wait_ge(S.stc, 16)
+    g.sync.wait_ge(S.std, 16)
     g.wait_ge(S.sent, sent)

@@ -3,8 +3,12 @@ from concourse.mybir import AluOpType
 
 TK = 32
 NB = 16
-HALF = NB // 2 * TK
 QUART = NB // 4 * TK
+
+LOADS = ["d", "p", "c", "l"]
+ORDER1 = ["d", "c", "l"]
+GQ = ["f", "d", "x", "c", "l", "s"]
+ORDER2 = ["c", "l", "p", "d"]
 
 SCRATCH = {
     "f1s": ("sbuf", [128, 128], "bfloat16"),
@@ -15,15 +19,12 @@ SCRATCH = {
     "tr": ("sbuf", [128, QUART], "bfloat16"),
     "land": ("sbuf", [128, NB * TK], "bfloat16"),
     "yb": ("sbuf", [128, NB * TK], "bfloat16"),
-    "p1d": ("psum", [128, 512], "float32"),
-    "p1c": ("psum", [128, 512], "float32"),
-    "p1n": ("psum", [128, 512], "float32"),
-    "p2d": ("psum", [128, 512], "float32"),
-    "p2c": ("psum", [128, 512], "float32"),
-    "p2n": ("psum", [128, 512], "float32"),
 }
-SEMAPHORES = ["l_f1", "l_f2", "l_xd", "l_td", "l_xc", "l_tc", "l_xn", "l_tn", "m1d", "m1c", "m1n", "ud", "uc", "un", "own",
-              "trk", "arrc", "arrn", "arrd", "m2d", "m2c", "m2n", "yd", "yc", "yn", "std", "stc", "stn", "sent"]
+SEMAPHORES = ["l_f1", "l_f2", "own", "trk", "sent", "hf1", "hxt"]
+for _k in LOADS:
+    SCRATCH["p1" + _k] = ("psum", [128, 512], "float32")
+    SCRATCH["p2" + _k] = ("psum", [128, 512], "float32")
+    SEMAPHORES += [_s + _k for _s in ("lx", "lt", "m1", "u", "arr", "m2", "y", "st")]
 
 
 def _bits(mask):
@@ -43,6 +44,9 @@ def _place(c, cores, topo):
         by_host.setdefault(topo.host(d), []).append(d)
     here = by_host[topo.host(c)]
     p = {"k": here.index(c), "local": [d for d in here if d != c]}
+    idle = [d for d in range(max(cores) + 1) if d not in cores and topo.host(d) == topo.host(c)
+            and topo.chip(d) == topo.chip(c) and topo.die(d) != topo.die(c)]
+    p["helper"] = idle[p["k"]]
     for h, members in by_host.items():
         if h == topo.host(c):
             continue
@@ -58,8 +62,7 @@ def _place(c, cores, topo):
         assert r == list(range(r[0], r[0] + len(r)))
         return r[0] * TK
 
-    p["near0"], p["dg0"], p["cb0"], p["pl0"] = (first_col(here + p["plane"]), first_col(p["diag"]), first_col(p["cable"]),
-                                                first_col(p["plane"]))
+    p["col"] = {"d": first_col(p["diag"]), "c": first_col(p["cable"]), "p": first_col(p["plane"]), "l": first_col(here)}
     first, second = ("plane", "cable") if p["k"] % 2 == 0 else ("cable", "plane")
     p["relay"], p["beyond"], p["beyond0"] = p[first][p["k"]], p[second], first_col(p[second])
     return p
@@ -68,8 +71,10 @@ def _place(c, cores, topo):
 def _plan(c, cores, topo):
     p = _place(c, cores, topo)
     me = cores.index(c)
+    hp = p["helper"]
     off = _bits(topo.mask(c, p["relay"]))
     on = [e for e in _bits(topo.mask(c, p["local"][0])) if e not in off]
+    half = len(on) // 2
 
     def spread(dsts, engines, src, col0, dst_col, sem):
         n = 1
@@ -78,32 +83,36 @@ def _plan(c, cores, topo):
         return [(d, src, cores.index(d) * TK - col0, "land", dst_col, TK, engines[i * n:(i + 1) * n], sem)
                 for i, d in enumerate(dsts)]
 
-    trunk = [(p["relay"], "u", p["dg0"], "tr", 0, QUART, off, "trk")]
-    cable = spread(p["cable"], off, "u", 0, me * TK, "arrc")
-    near = spread(p["plane"], off, "u", 0, me * TK, "arrn") + spread(p["local"], on, "u", 0, me * TK, "arrn")
-    scatter = spread(p["beyond"], off, "tr", p["beyond0"], cores.index(p["relay"]) * TK, "arrd")
-    return [trunk, cable, near, scatter]
+    pc = p["col"]["p"]
+    return {"f": [(hp, "f1s", 0, "f1s", 0, 128, on, "hf1")],
+            "d": [(p["relay"], "u", p["col"]["d"], "tr", 0, QUART, off, "trk")],
+            "x": [(hp, "xs", pc, "xs", pc, QUART, on[:half], "hxt"), (hp, "ts", pc, "ts", pc, QUART, on[half:], "hxt")],
+            "c": spread(p["cable"], off, "u", 0, me * TK, "arrc"),
+            "l": spread(p["local"], on, "u", 0, me * TK, "arrl"),
+            "s": spread(p["beyond"], off, "tr", p["beyond0"], cores.index(p["relay"]) * TK, "arrd"),
+            "h": spread(p["plane"], _bits(topo.mask(hp, p["plane"][0])), "u", 0, me * TK, "arrp")}
 
 
 def rank_program(g, core, T, topo):
-    if T.rank_of(core) is None:
-        return
     cores = list(T.cores)
     S = T.sem
     pe, ve = g.tensor, g.vector
-    p = _place(core, cores, topo)
-    me = cores.index(core)
-    dg = slice(p["dg0"], p["dg0"] + QUART)
-    cb = slice(p["cb0"], p["cb0"] + QUART)
-    near = slice(p["near0"], p["near0"] + HALF)
-    calls = _plan(core, cores, topo)
-    expect = {"trk": 0, "arrc": 0, "arrn": 0, "arrd": 0}
+    owner = core if T.rank_of(core) is not None else None
+    if owner is None:
+        for r in cores:
+            if topo.host(r) == topo.host(core) and _place(r, cores, topo)["helper"] == core:
+                owner = r
+        if owner is None:
+            return
+    p = _place(owner, cores, topo)
+    sl = {k: slice(p["col"][k], p["col"][k] + QUART) for k in LOADS}
+    calls = _plan(owner, cores, topo)
+    expect = {}
     for d in cores:
-        if d != core:
-            for call in _plan(d, cores, topo):
-                for w in call:
-                    if w[0] == core:
-                        expect[w[7]] += len(w[6])
+        for call in _plan(d, cores, topo).values():
+            for w in call:
+                if w[0] == core:
+                    expect[w[7]] = expect.get(w[7], 0) + len(w[6])
 
     def issue(call):
         trs = []
@@ -114,66 +123,64 @@ def rank_program(g, core, T, topo):
         g.remote_dma_fused(trs, local_sem=S.sent)
         return sum(len(w[6]) for w in call)
 
+    def first_stage(k):
+        pe.matmul(T["p1" + k][:, 0:QUART], T.f1s[:], T.xs[:, sl[k]], start=True, stop=True).then_inc(S["m1" + k], 1)
+        ve.wait_ge(S["m1" + k], 1)
+
+    if owner != core:
+        pe.wait_ge(S.hf1, expect["hf1"])
+        pe.wait_ge(S.hxt, expect["hxt"])
+        first_stage("p")
+        ve.wait_ge(S.hxt, expect["hxt"])
+        ve.tensor_tensor(T.u[:, sl["p"]], T.p1p[:, 0:QUART], T.ts[:, sl["p"]], AluOpType.mult).then_inc(S.up, 1)
+        g.wait_ge(S.up, 1)
+        g.wait_ge(S.sent, issue(calls["h"]))
+        return
+
+    me = cores.index(core)
     g.sync.dma_start(T.f1s[:], T.f1[:]).then_inc(S.l_f1, 16)
-    g.scalar.dma_start(T.xs[:, dg], T.x[:, dg]).then_inc(S.l_xd, 16)
-    g.sync.dma_start(T.ts[:, dg], T.t[:, dg]).then_inc(S.l_td, 16)
-    g.scalar.dma_start(T.xs[:, cb], T.x[:, cb]).then_inc(S.l_xc, 16)
-    g.sync.dma_start(T.ts[:, cb], T.t[:, cb]).then_inc(S.l_tc, 16)
-    g.scalar.dma_start(T.xs[:, near], T.x[:, near]).then_inc(S.l_xn, 16)
-    g.sync.dma_start(T.ts[:, near], T.t[:, near]).then_inc(S.l_tn, 16)
+    for k in LOADS:
+        g.scalar.dma_start(T.xs[:, sl[k]], T.x[:, sl[k]]).then_inc(S["lx" + k], 16)
+        g.sync.dma_start(T.ts[:, sl[k]], T.t[:, sl[k]]).then_inc(S["lt" + k], 16)
     g.scalar.dma_start(T.f2s[:], T.f2[:]).then_inc(S.l_f2, 16)
 
     pe.wait_ge(S.l_f1, 16)
-    pe.wait_ge(S.l_xd, 16)
-    pe.matmul(T.p1d[:, 0:QUART], T.f1s[:], T.xs[:, dg], start=True, stop=True).then_inc(S.m1d, 1)
-    pe.wait_ge(S.l_xc, 16)
-    pe.matmul(T.p1c[:, 0:QUART], T.f1s[:], T.xs[:, cb], start=True, stop=True).then_inc(S.m1c, 1)
-    pe.wait_ge(S.l_xn, 16)
-    pe.matmul(T.p1n[:, 0:HALF], T.f1s[:], T.xs[:, near], start=True, stop=True).then_inc(S.m1n, 1)
-    ve.wait_ge(S.m1d, 1)
-    ve.wait_ge(S.l_td, 16)
-    ve.tensor_tensor(T.u[:, dg], T.p1d[:, 0:QUART], T.ts[:, dg], AluOpType.mult).then_inc(S.ud, 1)
-    ve.wait_ge(S.m1c, 1)
-    ve.wait_ge(S.l_tc, 16)
-    ve.tensor_tensor(T.u[:, cb], T.p1c[:, 0:QUART], T.ts[:, cb], AluOpType.mult).then_inc(S.uc, 1)
-    ve.wait_ge(S.m1n, 1)
-    ve.wait_ge(S.l_tn, 16)
-    ve.tensor_tensor(T.u[:, near], T.p1n[:, 0:HALF], T.ts[:, near], AluOpType.mult).then_inc(S.un, 1)
     o = me * TK
-    ve.tensor_tensor(T.land[:, o:o + TK], T.p1n[:, o - p["near0"]:o - p["near0"] + TK], T.ts[:, o:o + TK],
-                     AluOpType.mult).then_inc(S.own, 1)
+    for k in ORDER1:
+        pe.wait_ge(S["lx" + k], 16)
+        first_stage(k)
+        ve.wait_ge(S["lt" + k], 16)
+        ve.tensor_tensor(T.u[:, sl[k]], T["p1" + k][:, 0:QUART], T.ts[:, sl[k]], AluOpType.mult).then_inc(S["u" + k], 1)
+        if k == "l":
+            q = o - sl[k].start
+            ve.tensor_tensor(T.land[:, o:o + TK], T["p1" + k][:, q:q + TK], T.ts[:, o:o + TK],
+                             AluOpType.mult).then_inc(S.own, 1)
 
     sent = 0
-    g.wait_ge(S.ud, 1)
-    sent += issue(calls[0])
-    g.wait_ge(S.uc, 1)
-    sent += issue(calls[1])
-    g.wait_ge(S.un, 1)
-    sent += issue(calls[2])
-    g.wait_ge(S.trk, expect["trk"])
-    sent += issue(calls[3])
+    for k in GQ:
+        if k == "f":
+            g.wait_ge(S.l_f1, 16)
+        elif k == "x":
+            g.wait_ge(S.lxp, 16)
+            g.wait_ge(S.ltp, 16)
+        elif k == "s":
+            g.wait_ge(S.trk, expect["trk"])
+        else:
+            g.wait_ge(S["u" + k], 1)
+        sent += issue(calls[k])
 
     pe.wait_ge(S.l_f2, 16)
-    pe.wait_ge(S.arrc, expect["arrc"])
-    pe.matmul(T.p2c[:, 0:QUART], T.f2s[:], T.land[:, cb], start=True, stop=True).then_inc(S.m2c, 1)
-    pe.wait_ge(S.own, 1)
-    pe.wait_ge(S.arrn, expect["arrn"])
-    pe.matmul(T.p2n[:, 0:HALF], T.f2s[:], T.land[:, near], start=True, stop=True).then_inc(S.m2n, 1)
-    pe.wait_ge(S.arrd, expect["arrd"])
-    pe.matmul(T.p2d[:, 0:QUART], T.f2s[:], T.land[:, dg], start=True, stop=True).then_inc(S.m2d, 1)
-    ve.wait_ge(S.m2c, 1)
-    ve.tensor_copy(T.yb[:, cb], T.p2c[:, 0:QUART]).then_inc(S.yc, 1)
-    ve.wait_ge(S.m2n, 1)
-    ve.tensor_copy(T.yb[:, near], T.p2n[:, 0:HALF]).then_inc(S.yn, 1)
-    ve.wait_ge(S.m2d, 1)
-    ve.tensor_copy(T.yb[:, dg], T.p2d[:, 0:QUART]).then_inc(S.yd, 1)
-    g.sync.wait_ge(S.yc, 1)
-    g.sync.dma_start(T.y[:, cb], T.yb[:, cb]).then_inc(S.stc, 16)
-    g.scalar.wait_ge(S.yn, 1)
-    g.scalar.dma_start(T.y[:, near], T.yb[:, near]).then_inc(S.stn, 16)
-    g.sync.wait_ge(S.yd, 1)
-    g.sync.dma_start(T.y[:, dg], T.yb[:, dg]).then_inc(S.std, 16)
-    g.scalar.wait_ge(S.stn, 16)
-    g.sync.wait_ge(S.stc, 16)
-    g.sync.wait_ge(S.std, 16)
+    queues = [g.sync, g.scalar]
+    for i, k in enumerate(ORDER2):
+        if k == "l":
+            pe.wait_ge(S.own, 1)
+        pe.wait_ge(S["arr" + k], expect["arr" + k])
+        pe.matmul(T["p2" + k][:, 0:QUART], T.f2s[:], T.land[:, sl[k]], start=True, stop=True).then_inc(S["m2" + k], 1)
+        ve.wait_ge(S["m2" + k], 1)
+        ve.tensor_copy(T.yb[:, sl[k]], T["p2" + k][:, 0:QUART]).then_inc(S["y" + k], 1)
+        q = queues[i % 2]
+        q.wait_ge(S["y" + k], 1)
+        q.dma_start(T.y[:, sl[k]], T.yb[:, sl[k]]).then_inc(S["st" + k], 16)
+    for i, k in enumerate(ORDER2):
+        queues[i % 2].wait_ge(S["st" + k], 16)
     g.wait_ge(S.sent, sent)

@@ -6,9 +6,10 @@ NB = 16
 QUART = NB // 4 * TK
 
 LOADS = ["d", "p", "c", "l"]
-ORDER1 = ["d", "c", "l"]
-GQ = ["f", "d", "x", "c", "l", "s"]
-ORDER2 = ["c", "l", "p", "d"]
+ORDER1 = ["d", "p", "a", "l"]
+GQ = ["f", "d", "p", "xb", "a", "l", "s"]
+ORDER2 = ["l", "p", "c", "d"]
+BANK = {"d": "p1d", "a": "p1a", "l": "p1l", "b": "p1a", "p": "p1p"}
 
 SCRATCH = {
     "f1s": ("sbuf", [128, 128], "bfloat16"),
@@ -19,12 +20,17 @@ SCRATCH = {
     "tr": ("sbuf", [128, QUART], "bfloat16"),
     "land": ("sbuf", [128, NB * TK], "bfloat16"),
     "yb": ("sbuf", [128, NB * TK], "bfloat16"),
+    "p1d": ("psum", [128, 512], "float32"),
+    "p1a": ("psum", [128, 512], "float32"),
+    "p1l": ("psum", [128, 512], "float32"),
+    "p1p": ("psum", [128, 512], "float32"),
 }
-SEMAPHORES = ["l_f1", "l_f2", "own", "trk", "sent", "hf1", "hxt"]
+SEMAPHORES = ["l_f1", "l_f2", "own", "trk", "sent", "hf1", "hxb", "hup"]
 for _k in LOADS:
-    SCRATCH["p1" + _k] = ("psum", [128, 512], "float32")
     SCRATCH["p2" + _k] = ("psum", [128, 512], "float32")
-    SEMAPHORES += [_s + _k for _s in ("lx", "lt", "m1", "u", "arr", "m2", "y", "st")]
+    SEMAPHORES += [_s + _k for _s in ("lx", "lt", "arr", "m2", "y", "st")]
+for _k in BANK:
+    SEMAPHORES += ["m1" + _k, "u" + _k]
 
 
 def _bits(mask):
@@ -62,7 +68,10 @@ def _place(c, cores, topo):
         assert r == list(range(r[0], r[0] + len(r)))
         return r[0] * TK
 
-    p["col"] = {"d": first_col(p["diag"]), "c": first_col(p["cable"]), "p": first_col(p["plane"]), "l": first_col(here)}
+    n = len(p["cable"]) // 2
+    p["cb_help"], p["cb_own"] = (p["cable"][:n], p["cable"][n:]) if p["k"] % 2 == 0 else (p["cable"][n:], p["cable"][:n])
+    p["col"] = {"d": (first_col(p["diag"]), QUART), "c": (first_col(p["cable"]), QUART), "p": (first_col(p["plane"]), QUART),
+                "l": (first_col(here), QUART), "a": (first_col(p["cb_own"]), n * TK), "b": (first_col(p["cb_help"]), n * TK)}
     first, second = ("plane", "cable") if p["k"] % 2 == 0 else ("cable", "plane")
     p["relay"], p["beyond"], p["beyond0"] = p[first][p["k"]], p[second], first_col(p[second])
     return p
@@ -74,6 +83,7 @@ def _plan(c, cores, topo):
     hp = p["helper"]
     off = _bits(topo.mask(c, p["relay"]))
     on = [e for e in _bits(topo.mask(c, p["local"][0])) if e not in off]
+    hoff = _bits(topo.mask(hp, p["plane"][0]))
     half = len(on) // 2
 
     def spread(dsts, engines, src, col0, dst_col, sem):
@@ -83,14 +93,18 @@ def _plan(c, cores, topo):
         return [(d, src, cores.index(d) * TK - col0, "land", dst_col, TK, engines[i * n:(i + 1) * n], sem)
                 for i, d in enumerate(dsts)]
 
-    pc = p["col"]["p"]
+    def raw(k, sem):
+        c0, n = p["col"][k]
+        return [(hp, "xs", c0, "xs", c0, n, on[:half], sem), (hp, "ts", c0, "ts", c0, n, on[half:], sem)]
+
     return {"f": [(hp, "f1s", 0, "f1s", 0, 128, on, "hf1")],
-            "d": [(p["relay"], "u", p["col"]["d"], "tr", 0, QUART, off, "trk")],
-            "x": [(hp, "xs", pc, "xs", pc, QUART, on[:half], "hxt"), (hp, "ts", pc, "ts", pc, QUART, on[half:], "hxt")],
-            "c": spread(p["cable"], off, "u", 0, me * TK, "arrc"),
+            "d": [(p["relay"], "u", p["col"]["d"][0], "tr", 0, QUART, off, "trk")],
+            "xb": raw("b", "hxb"), "p": [(hp, "u", p["col"]["p"][0], "u", p["col"]["p"][0], QUART, on, "hup")],
+            "a": spread(p["cb_own"], off, "u", 0, me * TK, "arrc"),
             "l": spread(p["local"], on, "u", 0, me * TK, "arrl"),
             "s": spread(p["beyond"], off, "tr", p["beyond0"], cores.index(p["relay"]) * TK, "arrd"),
-            "h": spread(p["plane"], _bits(topo.mask(hp, p["plane"][0])), "u", 0, me * TK, "arrp")}
+            "hb": spread(p["cb_help"], hoff, "u", 0, me * TK, "arrc"),
+            "hp": spread(p["plane"], hoff, "u", 0, me * TK, "arrp")}
 
 
 def rank_program(g, core, T, topo):
@@ -105,7 +119,8 @@ def rank_program(g, core, T, topo):
         if owner is None:
             return
     p = _place(owner, cores, topo)
-    sl = {k: slice(p["col"][k], p["col"][k] + QUART) for k in LOADS}
+    sl = {k: slice(v[0], v[0] + v[1]) for k, v in p["col"].items()}
+    wd = {k: v[1] for k, v in p["col"].items()}
     calls = _plan(owner, cores, topo)
     expect = {}
     for d in cores:
@@ -123,18 +138,22 @@ def rank_program(g, core, T, topo):
         g.remote_dma_fused(trs, local_sem=S.sent)
         return sum(len(w[6]) for w in call)
 
-    def first_stage(k):
-        pe.matmul(T["p1" + k][:, 0:QUART], T.f1s[:], T.xs[:, sl[k]], start=True, stop=True).then_inc(S["m1" + k], 1)
+    def first_stage(k, t_sem, t_count):
+        bank = T[BANK[k]]
+        pe.matmul(bank[:, 0:wd[k]], T.f1s[:], T.xs[:, sl[k]], start=True, stop=True).then_inc(S["m1" + k], 1)
         ve.wait_ge(S["m1" + k], 1)
+        ve.wait_ge(t_sem, t_count)
+        ve.tensor_tensor(T.u[:, sl[k]], bank[:, 0:wd[k]], T.ts[:, sl[k]], AluOpType.mult).then_inc(S["u" + k], 1)
 
     if owner != core:
         pe.wait_ge(S.hf1, expect["hf1"])
-        pe.wait_ge(S.hxt, expect["hxt"])
-        first_stage("p")
-        ve.wait_ge(S.hxt, expect["hxt"])
-        ve.tensor_tensor(T.u[:, sl["p"]], T.p1p[:, 0:QUART], T.ts[:, sl["p"]], AluOpType.mult).then_inc(S.up, 1)
-        g.wait_ge(S.up, 1)
-        g.wait_ge(S.sent, issue(calls["h"]))
+        pe.wait_ge(S.hxb, expect["hxb"])
+        first_stage("b", S.hxb, expect["hxb"])
+        g.wait_ge(S.hup, expect["hup"])
+        sent = issue(calls["hp"])
+        g.wait_ge(S.ub, 1)
+        sent += issue(calls["hb"])
+        g.wait_ge(S.sent, sent)
         return
 
     me = cores.index(core)
@@ -146,23 +165,22 @@ def rank_program(g, core, T, topo):
 
     pe.wait_ge(S.l_f1, 16)
     o = me * TK
+    src = {"d": "d", "a": "c", "l": "l", "b": "c", "p": "p"}
     for k in ORDER1:
-        pe.wait_ge(S["lx" + k], 16)
-        first_stage(k)
-        ve.wait_ge(S["lt" + k], 16)
-        ve.tensor_tensor(T.u[:, sl[k]], T["p1" + k][:, 0:QUART], T.ts[:, sl[k]], AluOpType.mult).then_inc(S["u" + k], 1)
+        pe.wait_ge(S["lx" + src[k]], 16)
+        first_stage(k, S["lt" + src[k]], 16)
         if k == "l":
             q = o - sl[k].start
-            ve.tensor_tensor(T.land[:, o:o + TK], T["p1" + k][:, q:q + TK], T.ts[:, o:o + TK],
+            ve.tensor_tensor(T.land[:, o:o + TK], T[BANK[k]][:, q:q + TK], T.ts[:, o:o + TK],
                              AluOpType.mult).then_inc(S.own, 1)
 
     sent = 0
     for k in GQ:
         if k == "f":
             g.wait_ge(S.l_f1, 16)
-        elif k == "x":
-            g.wait_ge(S.lxp, 16)
-            g.wait_ge(S.ltp, 16)
+        elif k[0] == "x":
+            g.wait_ge(S["lx" + src[k[1]]], 16)
+            g.wait_ge(S["lt" + src[k[1]]], 16)
         elif k == "s":
             g.wait_ge(S.trk, expect["trk"])
         else:

from concourse.bass import DstId, RemoteDMATransfer
from concourse.mybir import AluOpType

TK = 32
NB = 16
QUART = NB // 4 * TK

LOADS = ["d", "p", "c", "l"]
ORDER1 = ["d", "p", "a", "l"]
GQ = ["f", "d", "p", "xb", "a", "l", "s"]
ORDER2 = ["l", "p", "c", "d"]
BANK = {"d": "p1d", "a": "p1a", "l": "p1l", "b": "p1a", "p": "p1p"}

SCRATCH = {
    "f1s": ("sbuf", [128, 128], "bfloat16"),
    "f2s": ("sbuf", [128, 128], "bfloat16"),
    "xs": ("sbuf", [128, NB * TK], "bfloat16"),
    "ts": ("sbuf", [128, NB * TK], "bfloat16"),
    "u": ("sbuf", [128, NB * TK], "bfloat16"),
    "tr": ("sbuf", [128, QUART], "bfloat16"),
    "land": ("sbuf", [128, NB * TK], "bfloat16"),
    "yb": ("sbuf", [128, NB * TK], "bfloat16"),
    "p1d": ("psum", [128, 512], "float32"),
    "p1a": ("psum", [128, 512], "float32"),
    "p1l": ("psum", [128, 512], "float32"),
    "p1p": ("psum", [128, 512], "float32"),
}
SEMAPHORES = ["l_f1", "l_f2", "own", "trk", "sent", "hf1", "hxb", "hup"]
for _k in LOADS:
    SCRATCH["p2" + _k] = ("psum", [128, 512], "float32")
    SEMAPHORES += [_s + _k for _s in ("lx", "lt", "arr", "m2", "y", "st")]
for _k in BANK:
    SEMAPHORES += ["m1" + _k, "u" + _k]


def _bits(mask):
    return [e for e in range(mask.bit_length()) if (mask >> e) & 1]


def _mask(engines):
    m = 0
    for e in engines:
        m |= 1 << e
    return m


def _place(c, cores, topo):
    by_host = {}
    for d in cores:
        by_host.setdefault(topo.host(d), []).append(d)
    here = by_host[topo.host(c)]
    p = {"k": here.index(c), "local": [d for d in here if d != c]}
    idle = [d for d in range(max(cores) + 1) if d not in cores and topo.host(d) == topo.host(c)
            and topo.chip(d) == topo.chip(c) and topo.die(d) != topo.die(c)]
    p["helper"] = idle[p["k"]]
    for h, members in by_host.items():
        if h == topo.host(c):
            continue
        if not topo.may_write(c, members[0]):
            p["diag"] = members
        elif topo.same_plane(c, members[0]):
            p["plane"] = members
        else:
            p["cable"] = members

    def first_col(members):
        r = sorted(cores.index(d) for d in members)
        assert r == list(range(r[0], r[0] + len(r)))
        return r[0] * TK

    n = len(p["cable"]) // 2
    p["cb_help"], p["cb_own"] = (p["cable"][:n], p["cable"][n:]) if p["k"] % 2 == 0 else (p["cable"][n:], p["cable"][:n])
    p["col"] = {"d": (first_col(p["diag"]), QUART), "c": (first_col(p["cable"]), QUART), "p": (first_col(p["plane"]), QUART),
                "l": (first_col(here), QUART), "a": (first_col(p["cb_own"]), n * TK), "b": (first_col(p["cb_help"]), n * TK)}
    first, second = ("plane", "cable") if p["k"] % 2 == 0 else ("cable", "plane")
    p["relay"], p["beyond"], p["beyond0"] = p[first][p["k"]], p[second], first_col(p[second])
    return p


def _plan(c, cores, topo):
    p = _place(c, cores, topo)
    me = cores.index(c)
    hp = p["helper"]
    off = _bits(topo.mask(c, p["relay"]))
    on = [e for e in _bits(topo.mask(c, p["local"][0])) if e not in off]
    hoff = _bits(topo.mask(hp, p["plane"][0]))
    half = len(on) // 2

    def spread(dsts, engines, src, col0, dst_col, sem):
        n = 1
        while n * 2 * len(dsts) <= len(engines):
            n *= 2
        return [(d, src, cores.index(d) * TK - col0, "land", dst_col, TK, engines[i * n:(i + 1) * n], sem)
                for i, d in enumerate(dsts)]

    def raw(k, sem):
        c0, n = p["col"][k]
        return [(hp, "xs", c0, "xs", c0, n, on[:half], sem), (hp, "ts", c0, "ts", c0, n, on[half:], sem)]

    return {"f": [(hp, "f1s", 0, "f1s", 0, 128, on, "hf1")],
            "d": [(p["relay"], "u", p["col"]["d"][0], "tr", 0, QUART, off, "trk")],
            "xb": raw("b", "hxb"), "p": [(hp, "u", p["col"]["p"][0], "u", p["col"]["p"][0], QUART, on, "hup")],
            "a": spread(p["cb_own"], off, "u", 0, me * TK, "arrc"),
            "l": spread(p["local"], on, "u", 0, me * TK, "arrl"),
            "s": spread(p["beyond"], off, "tr", p["beyond0"], cores.index(p["relay"]) * TK, "arrd"),
            "hb": spread(p["cb_help"], hoff, "u", 0, me * TK, "arrc"),
            "hp": spread(p["plane"], hoff, "u", 0, me * TK, "arrp")}


def rank_program(g, core, T, topo):
    cores = list(T.cores)
    S = T.sem
    pe, ve = g.tensor, g.vector
    owner = core if T.rank_of(core) is not None else None
    if owner is None:
        for r in cores:
            if topo.host(r) == topo.host(core) and _place(r, cores, topo)["helper"] == core:
                owner = r
        if owner is None:
            return
    p = _place(owner, cores, topo)
    sl = {k: slice(v[0], v[0] + v[1]) for k, v in p["col"].items()}
    wd = {k: v[1] for k, v in p["col"].items()}
    calls = _plan(owner, cores, topo)
    expect = {}
    for d in cores:
        for call in _plan(d, cores, topo).values():
            for w in call:
                if w[0] == core:
                    expect[w[7]] = expect.get(w[7], 0) + len(w[6])

    def issue(call):
        trs = []
        for (d, sb, sc, db, dc, n, engines, sem) in call:
            rid, pid = topo.addr(d, core)
            trs.append(RemoteDMATransfer(dst_ids=[DstId(rid=rid, pnc=pid)], dma_engine_mask=_mask(engines),
                                         remote_sem=S[sem], src=T[sb][:, sc:sc + n], dst=T[db][:, dc:dc + n]))
        g.remote_dma_fused(trs, local_sem=S.sent)
        return sum(len(w[6]) for w in call)

    def first_stage(k, t_sem, t_count):
        bank = T[BANK[k]]
        pe.matmul(bank[:, 0:wd[k]], T.f1s[:], T.xs[:, sl[k]], start=True, stop=True).then_inc(S["m1" + k], 1)
        ve.wait_ge(S["m1" + k], 1)
        ve.wait_ge(t_sem, t_count)
        ve.tensor_tensor(T.u[:, sl[k]], bank[:, 0:wd[k]], T.ts[:, sl[k]], AluOpType.mult).then_inc(S["u" + k], 1)

    if owner != core:
        pe.wait_ge(S.hf1, expect["hf1"])
        pe.wait_ge(S.hxb, expect["hxb"])
        first_stage("b", S.hxb, expect["hxb"])
        g.wait_ge(S.hup, expect["hup"])
        sent = issue(calls["hp"])
        g.wait_ge(S.ub, 1)
        sent += issue(calls["hb"])
        g.wait_ge(S.sent, sent)
        return

    me = cores.index(core)
    g.sync.dma_start(T.f1s[:], T.f1[:]).then_inc(S.l_f1, 16)
    for k in LOADS:
        g.scalar.dma_start(T.xs[:, sl[k]], T.x[:, sl[k]]).then_inc(S["lx" + k], 16)
        g.sync.dma_start(T.ts[:, sl[k]], T.t[:, sl[k]]).then_inc(S["lt" + k], 16)
    g.scalar.dma_start(T.f2s[:], T.f2[:]).then_inc(S.l_f2, 16)

    pe.wait_ge(S.l_f1, 16)
    o = me * TK
    src = {"d": "d", "a": "c", "l": "l", "b": "c", "p": "p"}
    for k in ORDER1:
        pe.wait_ge(S["lx" + src[k]], 16)
        first_stage(k, S["lt" + src[k]], 16)
        if k == "l":
            q = o - sl[k].start
            ve.tensor_tensor(T.land[:, o:o + TK], T[BANK[k]][:, q:q + TK], T.ts[:, o:o + TK],
                             AluOpType.mult).then_inc(S.own, 1)

    sent = 0
    for k in GQ:
        if k == "f":
            g.wait_ge(S.l_f1, 16)
        elif k[0] == "x":
            g.wait_ge(S["lx" + src[k[1]]], 16)
            g.wait_ge(S["lt" + src[k[1]]], 16)
        elif k == "s":
            g.wait_ge(S.trk, expect["trk"])
        else:
            g.wait_ge(S["u" + k], 1)
        sent += issue(calls[k])

    pe.wait_ge(S.l_f2, 16)
    queues = [g.sync, g.scalar]
    for i, k in enumerate(ORDER2):
        if k == "l":
            pe.wait_ge(S.own, 1)
        pe.wait_ge(S["arr" + k], expect["arr" + k])
        pe.matmul(T["p2" + k][:, 0:QUART], T.f2s[:], T.land[:, sl[k]], start=True, stop=True).then_inc(S["m2" + k], 1)
        ve.wait_ge(S["m2" + k], 1)
        ve.tensor_copy(T.yb[:, sl[k]], T["p2" + k][:, 0:QUART]).then_inc(S["y" + k], 1)
        q = queues[i % 2]
        q.wait_ge(S["y" + k], 1)
        q.dma_start(T.y[:, sl[k]], T.yb[:, sl[k]]).then_inc(S["st" + k], 16)
    for i, k in enumerate(ORDER2):
        queues[i % 2].wait_ge(S["st" + k], 16)
    g.wait_ge(S.sent, sent)
